import numpy as np
import ml_dtypes


def mxq(x, axis, fmt="e4m3"):
    dtype, down = {"e4m3": (ml_dtypes.float8_e4m3fn, 7), "e5m2": (ml_dtypes.float8_e5m2, 14)}[fmt]
    v = np.moveaxis(np.asarray(x, np.float32).astype(ml_dtypes.bfloat16).astype(np.float64), axis, -1)
    blocks = v.reshape(v.shape[:-1] + (-1, 32))
    amax = np.abs(blocks).max(-1, keepdims=True)
    byte = np.maximum(np.where(amax > 0, np.frexp(amax)[1] - 1 + 127, 0) - down, 1)
    scale = np.exp2(byte - 127.0)
    codes = (blocks / scale).astype(np.float32).astype(dtype).astype(np.float64)
    return np.moveaxis((codes * scale).reshape(v.shape), -1, axis)


WIDE = False


def mx_kscale(k):
    if not WIDE:
        return np.ones(k)
    levels = np.array([10, -10, 5, -5, 0])
    if k % 512:
        return np.exp2(np.random.permutation(np.resize(levels, k // 32))).repeat(32)
    a = np.empty((k // 512, 16))
    for p in range(k // 512):
        a[p, :8] = np.random.permutation(np.resize(levels, 8))
        for g in range(8):
            far = levels[np.abs(levels - a[p, g]) >= 10]
            a[p, g + 8] = far[np.random.randint(len(far))]
    return np.exp2(a.ravel()).repeat(32)


def f64(x):
    return np.asarray(x).astype(np.float64)


def striped8(idx):
    return np.asarray(idx).reshape(8, -1, 16).transpose(0, 2, 1).reshape(128, -1).astype(np.uint16)


def unstriped8(offs):
    return offs.reshape(8, 16, -1).transpose(0, 2, 1).reshape(8, -1).astype(np.int64)


def pick8(x, idx, run):
    r = np.arange(len(x))
    return x[r[:, None], idx[r % (8 * run) // run]]


E2M1 = np.array([0.0, 0.5, 1.0, 1.5, 2.0, 3.0, 4.0, 6.0, -0.0, -0.5, -1.0, -1.5, -2.0, -3.0, -4.0, -6.0])


def pack_weight(w, fmt):
    k, n = w.shape
    w = f64(np.asarray(w, np.float32).astype(ml_dtypes.bfloat16)).reshape(k // 32, 32, n)
    amax = np.abs(w).max(1)
    if fmt == "e4m3":
        byte = np.frexp(amax)[1] - 1 + 127 - 7
    else:
        mant, ex = np.frexp(amax / 6.0)
        byte = np.where(mant > 0.5, ex, ex - 1) + 127
    byte = np.clip(np.where(amax > 0, byte, 1), 1, 254)
    scaled = (w * np.exp2(127.0 - byte)[:, None, :]).reshape(k, n).astype(np.float32)
    by_word = np.ascontiguousarray(scaled.reshape(k // 512, 128, 4, n).transpose(0, 1, 3, 2))
    if fmt == "e4m3":
        words = by_word.astype(ml_dtypes.float8_e4m3fn).view(np.uint8)
    else:
        c = by_word.astype(ml_dtypes.float4_e2m1fn).view(np.uint8) & 0xF
        words = (c[..., 0::2] | (c[..., 1::2] << 4)).reshape(k // 512, 128, 2 * n)
    return np.ascontiguousarray(words), np.ascontiguousarray(byte.astype(np.uint8).reshape(k // 512, 16, n))


def unpack_weight(words, scales, fmt):
    g, _, n = scales.shape
    words = np.ascontiguousarray(words).reshape(g, 128, n, -1)
    if fmt == "e4m3":
        vals = words.view(ml_dtypes.float8_e4m3fn).astype(np.float64)
    else:
        nib = np.empty((g, 128, n, 4), np.uint8)
        nib[..., 0::2] = words & 0xF
        nib[..., 1::2] = words >> 4
        vals = E2M1[nib]
    vals = vals * np.repeat(np.exp2(scales.astype(np.float64) - 127.0), 8, axis=1)[..., None]
    return vals.transpose(0, 1, 3, 2).reshape(g * 512, n)


D, T, I, Q = 512, 1024, 512, 128


def setup_inputs():
    n = np.random.standard_normal
    idx = np.stack([np.random.permutation(T)[:I] for _ in range(8)])
    idx2 = np.stack([np.random.permutation(T)[:I] for _ in range(8)])
    idx3 = np.stack([np.random.permutation(T)[:I] for _ in range(8)])
    idx4 = np.stack([np.random.permutation(T)[:I] for _ in range(8)])
    fd = mx_kscale(D)
    keysp = pack_weight(n((D, T)) / fd[:, None], "e2m1")
    return {
        "query": (n((D, Q)) * 1.1 / np.sqrt(D) * fd[:, None]).astype(np.float32),
        "keys_words": keysp[0],
        "keys_scales": keysp[1],
        "lam": (np.random.uniform(0.8, 1.5, (Q, 1))).astype(np.float32),
        "old": (1.0 * n((Q, T))).astype(np.float32),
        "offs": striped8(idx),
        "offs2": striped8(idx2),
        "offs3": striped8(idx3),
        "offs4": striped8(idx4),
    }


def reference(query, keys_words, keys_scales, lam, old, offs, offs2, offs3, offs4):
    idx = unstriped8(offs)
    idx2 = unstriped8(offs2)
    idx3 = unstriped8(offs3)
    idx4 = unstriped8(offs4)
    keysu = unpack_weight(keys_words, keys_scales, "e2m1")
    queryq = mxq(f64(query), 0, "e4m3")
    a = queryq.T @ keysu
    lo2 = np.minimum(pick8(a, idx2, 16), pick8(a, idx3, 16)) - 0.5
    hi2 = np.maximum(pick8(a, idx2, 16), pick8(a, idx3, 16)) + 0.5
    w = (pick8(a, idx, 16) - np.maximum(lo2, np.minimum(hi2, pick8(a, idx, 16))) * 0.5) * f64(lam)
    f1 = np.zeros((Q, T))
    f1[np.arange(Q)[:, None], idx4[np.arange(Q) % 128 // 16]] = w
    y = f64(old) + f1
    return y

@@ -1,0 +1,130 @@
+from contextlib import ExitStack
+
+import concourse.mybir as mybir
+
+D, T, SLOTS, Q = 512, 1024, 512, 128
+FLOPS = 2 * D * Q * T
+
+F32 = mybir.dt.float32
+BF16 = mybir.dt.bfloat16
+I32 = mybir.dt.int32
+U32 = mybir.dt.uint32
+U16 = mybir.dt.uint16
+U8 = mybir.dt.uint8
+FP8X4 = mybir.dt.float8_e4m3fn_x4
+FP4X4 = mybir.dt.float4_e2m1fn_x4
+ALU = mybir.AluOpType
+COPY = mybir.ActivationFunctionType.Copy
+
+P = 128
+PACK = 4
+PER_COLUMN = 16
+N_MM = 256
+HALF = SLOTS // 2
+N_OUT = 256
+MARGIN = 0.5
+LEAN = 0.5
+
+
+def tile_attend_heldbetween_lean_putold_heads_kernel(
+    tc, query, keys_words, keys_scales, lam, old, offs, offs2, offs3, offs4, out
+):
+    nc = tc.nc
+    with ExitStack() as ctx:
+        sb = ctx.enter_context(tc.tile_pool(name="sb", bufs=1))
+        ps = ctx.enter_context(tc.psum_pool(name="ps", bufs=1))
+
+        list_x = sb.tile([P, SLOTS // PER_COLUMN], U16, name="list_x")
+        list_u = sb.tile([P, SLOTS // PER_COLUMN], U16, name="list_u")
+        list_v = sb.tile([P, SLOTS // PER_COLUMN], U16, name="list_v")
+        list_put = sb.tile([P, SLOTS // PER_COLUMN], U16, name="list_put")
+        q_raw = sb.tile([P, PACK, Q], F32, name="q_raw")
+        k_words = sb.tile([P, 2 * T], U8, name="k_words", align_bytes=64)
+        k_scales = sb.tile([P, T], U8, name="k_scales", align_bytes=64)
+        lam_col = sb.tile([P, 1], F32, name="lam_col")
+        old_sb = sb.tile([P, T], F32, name="old_sb")
+        placed = sb.tile([P, T], F32, name="placed")
+
+        nc.vector.memset(k_scales[:].bitcast(I32), 0)
+        nc.vector.memset(placed[:], 0.0)
+
+        nc.sync.dma_start(out=q_raw[:], in_=query.rearrange("(p j) q -> p j q", j=PACK))
+        nc.sync.dma_start(out=k_words[:].bitcast(I32), in_=keys_words[0].bitcast(I32))
+        for quad in range(4):
+            nc.sync.dma_start(
+                out=k_scales[32 * quad : 32 * quad + 4, :].bitcast(I32),
+                in_=keys_scales[0, 4 * quad : 4 * quad + 4, :].bitcast(I32),
+            )
+        nc.sync.dma_start(list_u[:], offs2)
+        nc.sync.dma_start(list_v[:], offs3)
+        nc.sync.dma_start(list_x[:], offs)
+        nc.sync.dma_start(out=lam_col[:], in_=lam)
+        nc.sync.dma_start(list_put[:], offs4)
+        nc.sync.dma_start(out=old_sb[:], in_=old)
+
+        q_bf = sb.tile([P, Q, PACK], BF16, name="q_bf", align_bytes=64)
+        nc.vector.tensor_copy(
+            out=q_bf[:].rearrange("p (c i) j -> p c j i", i=4),
+            in_=q_raw[:].rearrange("p j (c i) -> p c j i", i=4),
+        )
+        q_codes = sb.tile([P, Q], U32, name="q_codes", align_bytes=64)
+        q_scales = sb.tile([P, Q], U8, name="q_scales", align_bytes=64)
+        nc.vector.quantize_mx(
+            out=q_codes[:].bitcast(FP8X4),
+            scales=q_scales[:],
+            in_=q_bf[:].rearrange("p q j -> p (q j)"),
+        )
+
+        a = sb.tile([P, T], F32, name="a")
+        for n in range(T // N_MM):
+            cols = slice(n * N_MM, (n + 1) * N_MM)
+            bank = ps.tile([P, N_MM], F32, name="bank%d" % n)
+            nc.tensor.matmul_mx(
+                out=bank[:],
+                lhsT=q_codes[:].bitcast(FP8X4),
+                lhsT_scale=q_scales[:],
+                rhs=k_words[:, 2 * n * N_MM : 2 * (n + 1) * N_MM].bitcast(FP4X4),
+                rhs_scale=k_scales[:, cols],
+                start=True,
+                stop=True,
+            )
+            if n % 2 == 0:
+                nc.scalar.activation(a[:, cols], bank[:], COPY)
+            else:
+                nc.vector.tensor_copy(out=a[:, cols], in_=bank[:])
+
+        halves = [slice(h * HALF, (h + 1) * HALF) for h in range(2)]
+        list_halves = [slice(h * HALF // PER_COLUMN, (h + 1) * HALF // PER_COLUMN) for h in range(2)]
+
+        u = sb.tile([P, SLOTS], F32, name="u")
+        v = sb.tile([P, SLOTS], F32, name="v")
+        x = sb.tile([P, SLOTS], F32, name="x")
+        x_lam = sb.tile([P, SLOTS], F32, name="x_lam")
+        nc.vector.tensor_copy(u[:], a[:].indirect(list_u[:]))
+        nc.scalar.activation(v[:], a[:].indirect(list_v[:]), COPY)
+        for h in range(2):
+            nc.scalar.activation(x[:, halves[h]], a[:].indirect(list_x[:, list_halves[h]]), COPY)
+        for h in range(2):
+            nc.scalar.activation(x_lam[:, halves[h]], x[:, halves[h]], COPY, scale=lam_col[:])
+
+        larger = sb.tile([P, SLOTS], F32, name="larger")
+        smaller = sb.tile([P, SLOTS], F32, name="smaller")
+        capped = sb.tile([P, SLOTS], F32, name="capped")
+        held = sb.tile([P, SLOTS], F32, name="held")
+        lean = sb.tile([P, SLOTS], F32, name="lean")
+        for s in halves:
+            nc.vector.tensor_tensor(larger[:, s], u[:, s], v[:, s], ALU.max)
+            nc.vector.tensor_tensor(smaller[:, s], u[:, s], v[:, s], ALU.min)
+        for s in halves:
+            nc.vector.scalar_tensor_tensor(capped[:, s], larger[:, s], MARGIN, x[:, s], ALU.add, ALU.min)
+        for s in halves:
+            nc.vector.scalar_tensor_tensor(held[:, s], smaller[:, s], -MARGIN, capped[:, s], ALU.add, ALU.max)
+        for s in halves:
+            nc.vector.tensor_scalar(lean[:, s], held[:, s], lam_col[:], -LEAN, ALU.mult, ALU.mult)
+        nc.vector.tensor_tensor(placed[:].indirect(list_put[:]), x_lam[:], lean[:], ALU.add)
+
+        total = sb.tile([P, T], F32, name="total")
+        for n in range(T // N_OUT):
+            cols = slice(n * N_OUT, (n + 1) * N_OUT)
+            nc.vector.tensor_tensor(total[:, cols], placed[:, cols], old_sb[:, cols], ALU.add)
+            nc.sync.dma_start(out=out[:, cols], in_=total[:, cols])

@@ -19,7 +19,7 @@ COPY = mybir.ActivationFunctionType.Copy
 P = 128
 PACK = 4
 PER_COLUMN = 16
-N_MM = 256
+MM_WIDTHS = (256, 256, 256, 128, 128)
 HALF = SLOTS // 2
 N_OUT = 256
 MARGIN = 0.5
@@ -76,19 +76,21 @@ def tile_attend_heldbetween_lean_putold_heads_kernel(
         )
 
         a = sb.tile([P, T], F32, name="a")
-        for n in range(T // N_MM):
-            cols = slice(n * N_MM, (n + 1) * N_MM)
-            bank = ps.tile([P, N_MM], F32, name="bank%d" % n)
+        first = 0
+        for n, width in enumerate(MM_WIDTHS):
+            cols = slice(first, first + width)
+            first = first + width
+            bank = ps.tile([P, width], F32, name="bank%d" % n)
             nc.tensor.matmul_mx(
                 out=bank[:],
                 lhsT=q_codes[:].bitcast(FP8X4),
                 lhsT_scale=q_scales[:],
-                rhs=k_words[:, 2 * n * N_MM : 2 * (n + 1) * N_MM].bitcast(FP4X4),
+                rhs=k_words[:, 2 * cols.start : 2 * cols.stop].bitcast(FP4X4),
                 rhs_scale=k_scales[:, cols],
                 start=True,
                 stop=True,
             )
-            if n % 2 == 0:
+            if n % 2 == 1:
                 nc.scalar.activation(a[:, cols], bank[:], COPY)
             else:
                 nc.vector.tensor_copy(out=a[:, cols], in_=bank[:])
@@ -100,8 +102,11 @@ def tile_attend_heldbetween_lean_putold_heads_kernel(
         v = sb.tile([P, SLOTS], F32, name="v")
         x = sb.tile([P, SLOTS], F32, name="x")
         x_lam = sb.tile([P, SLOTS], F32, name="x_lam")
-        nc.vector.tensor_copy(u[:], a[:].indirect(list_u[:]))
-        nc.scalar.activation(v[:], a[:].indirect(list_v[:]), COPY)
+        lean_col = sb.tile([P, 1], F32, name="lean_col")
+        nc.gpsimd.tensor_scalar(lean_col[:], lam_col[:], -LEAN, 0.0, ALU.mult, ALU.add)
+        for h in range(2):
+            nc.vector.tensor_copy(u[:, halves[h]], a[:].indirect(list_u[:, list_halves[h]]))
+            nc.scalar.activation(v[:, halves[h]], a[:].indirect(list_v[:, list_halves[h]]), COPY)
         for h in range(2):
             nc.scalar.activation(x[:, halves[h]], a[:].indirect(list_x[:, list_halves[h]]), COPY)
         for h in range(2):
@@ -112,16 +117,33 @@ def tile_attend_heldbetween_lean_putold_heads_kernel(
         capped = sb.tile([P, SLOTS], F32, name="capped")
         held = sb.tile([P, SLOTS], F32, name="held")
         lean = sb.tile([P, SLOTS], F32, name="lean")
-        for s in halves:
-            nc.vector.tensor_tensor(larger[:, s], u[:, s], v[:, s], ALU.max)
-            nc.vector.tensor_tensor(smaller[:, s], u[:, s], v[:, s], ALU.min)
-        for s in halves:
+
+        def pick(dst, s, op):
+            nc.vector.tensor_tensor(dst[:, s], u[:, s], v[:, s], op)
+
+        def cap(s):
             nc.vector.scalar_tensor_tensor(capped[:, s], larger[:, s], MARGIN, x[:, s], ALU.add, ALU.min)
-        for s in halves:
+
+        def hold(s):
             nc.vector.scalar_tensor_tensor(held[:, s], smaller[:, s], -MARGIN, capped[:, s], ALU.add, ALU.max)
-        for s in halves:
-            nc.vector.tensor_scalar(lean[:, s], held[:, s], lam_col[:], -LEAN, ALU.mult, ALU.mult)
-        nc.vector.tensor_tensor(placed[:].indirect(list_put[:]), x_lam[:], lean[:], ALU.add)
+
+        def put(h):
+            s = halves[h]
+            nc.vector.tensor_tensor(placed[:].indirect(list_put[:, list_halves[h]]), x_lam[:, s], lean[:, s], ALU.add)
+
+        early, late = halves
+        pick(larger, early, ALU.max)
+        pick(smaller, early, ALU.min)
+        pick(larger, late, ALU.max)
+        cap(early)
+        pick(smaller, late, ALU.min)
+        hold(early)
+        cap(late)
+        nc.vector.tensor_scalar(lean[:, early], held[:, early], lam_col[:], -LEAN, ALU.mult, ALU.mult)
+        hold(late)
+        put(0)
+        nc.scalar.activation(lean[:, late], held[:, late], COPY, scale=lean_col[:])
+        put(1)
 
         total = sb.tile([P, T], F32, name="total")
         for n in range(T // N_OUT):

@@ -20,6 +20,7 @@ P = 128
 PACK = 4
 PER_COLUMN = 16
 MM_WIDTHS = (256, 256, 256, 128, 128)
+CAST_SPLIT = 88
 HALF = SLOTS // 2
 N_OUT = 256
 MARGIN = 0.5
@@ -49,7 +50,9 @@ def tile_attend_heldbetween_lean_putold_heads_kernel(
         nc.vector.memset(placed[:], 0.0)
 
         nc.sync.dma_start(out=q_raw[:], in_=query.rearrange("(p j) q -> p j q", j=PACK))
-        nc.sync.dma_start(out=k_words[:].bitcast(I32), in_=keys_words[0].bitcast(I32))
+        for half in range(2):
+            span = slice(half * T, (half + 1) * T)
+            nc.sync.dma_start(out=k_words[:, span].bitcast(I32), in_=keys_words[0, :, span].bitcast(I32))
         for quad in range(4):
             nc.sync.dma_start(
                 out=k_scales[32 * quad : 32 * quad + 4, :].bitcast(I32),
@@ -58,14 +61,19 @@ def tile_attend_heldbetween_lean_putold_heads_kernel(
         nc.sync.dma_start(list_u[:], offs2)
         nc.sync.dma_start(list_v[:], offs3)
         nc.sync.dma_start(list_x[:], offs)
-        nc.sync.dma_start(out=lam_col[:], in_=lam)
+        nc.gpsimd.dma_start(out=lam_col[:], in_=lam)
         nc.sync.dma_start(list_put[:], offs4)
         nc.sync.dma_start(out=old_sb[:], in_=old)
 
         q_bf = sb.tile([P, Q, PACK], BF16, name="q_bf", align_bytes=64)
         nc.vector.tensor_copy(
-            out=q_bf[:].rearrange("p (c i) j -> p c j i", i=4),
-            in_=q_raw[:].rearrange("p j (c i) -> p c j i", i=4),
+            out=q_bf[:, :CAST_SPLIT, :].rearrange("p (c i) j -> p c j i", i=4),
+            in_=q_raw[:, :, :CAST_SPLIT].rearrange("p j (c i) -> p c j i", i=4),
+        )
+        nc.scalar.activation(
+            q_bf[:, CAST_SPLIT:, :].rearrange("p (c i) j -> p c j i", i=4),
+            q_raw[:, :, CAST_SPLIT:].rearrange("p j (c i) -> p c j i", i=4),
+            COPY,
         )
         q_codes = sb.tile([P, Q], U32, name="q_codes", align_bytes=64)
         q_scales = sb.tile([P, Q], U8, name="q_scales", align_bytes=64)
@@ -90,7 +98,7 @@ def tile_attend_heldbetween_lean_putold_heads_kernel(
                 start=True,
                 stop=True,
             )
-            if n % 2 == 1:
+            if n % 2 == 0:
                 nc.scalar.activation(a[:, cols], bank[:], COPY)
             else:
                 nc.vector.tensor_copy(out=a[:, cols], in_=bank[:])

from contextlib import ExitStack

import concourse.mybir as mybir

D, T, SLOTS, Q = 512, 1024, 512, 128
FLOPS = 2 * D * Q * T

F32 = mybir.dt.float32
BF16 = mybir.dt.bfloat16
I32 = mybir.dt.int32
U32 = mybir.dt.uint32
U16 = mybir.dt.uint16
U8 = mybir.dt.uint8
FP8X4 = mybir.dt.float8_e4m3fn_x4
FP4X4 = mybir.dt.float4_e2m1fn_x4
ALU = mybir.AluOpType
COPY = mybir.ActivationFunctionType.Copy

P = 128
PACK = 4
PER_COLUMN = 16
MM_WIDTHS = (256, 256, 256, 128, 128)
CAST_SPLIT = 88
HALF = SLOTS // 2
N_OUT = 256
MARGIN = 0.5
LEAN = 0.5


def tile_attend_heldbetween_lean_putold_heads_kernel(
    tc, query, keys_words, keys_scales, lam, old, offs, offs2, offs3, offs4, out
):
    nc = tc.nc
    with ExitStack() as ctx:
        sb = ctx.enter_context(tc.tile_pool(name="sb", bufs=1))
        ps = ctx.enter_context(tc.psum_pool(name="ps", bufs=1))

        list_x = sb.tile([P, SLOTS // PER_COLUMN], U16, name="list_x")
        list_u = sb.tile([P, SLOTS // PER_COLUMN], U16, name="list_u")
        list_v = sb.tile([P, SLOTS // PER_COLUMN], U16, name="list_v")
        list_put = sb.tile([P, SLOTS // PER_COLUMN], U16, name="list_put")
        q_raw = sb.tile([P, PACK, Q], F32, name="q_raw")
        k_words = sb.tile([P, 2 * T], U8, name="k_words", align_bytes=64)
        k_scales = sb.tile([P, T], U8, name="k_scales", align_bytes=64)
        lam_col = sb.tile([P, 1], F32, name="lam_col")
        old_sb = sb.tile([P, T], F32, name="old_sb")
        placed = sb.tile([P, T], F32, name="placed")

        nc.vector.memset(k_scales[:].bitcast(I32), 0)
        nc.vector.memset(placed[:], 0.0)

        nc.sync.dma_start(out=q_raw[:], in_=query.rearrange("(p j) q -> p j q", j=PACK))
        for half in range(2):
            span = slice(half * T, (half + 1) * T)
            nc.sync.dma_start(out=k_words[:, span].bitcast(I32), in_=keys_words[0, :, span].bitcast(I32))
        for quad in range(4):
            nc.sync.dma_start(
                out=k_scales[32 * quad : 32 * quad + 4, :].bitcast(I32),
                in_=keys_scales[0, 4 * quad : 4 * quad + 4, :].bitcast(I32),
            )
        nc.sync.dma_start(list_u[:], offs2)
        nc.sync.dma_start(list_v[:], offs3)
        nc.sync.dma_start(list_x[:], offs)
        nc.gpsimd.dma_start(out=lam_col[:], in_=lam)
        nc.sync.dma_start(list_put[:], offs4)
        nc.sync.dma_start(out=old_sb[:], in_=old)

        q_bf = sb.tile([P, Q, PACK], BF16, name="q_bf", align_bytes=64)
        nc.vector.tensor_copy(
            out=q_bf[:, :CAST_SPLIT, :].rearrange("p (c i) j -> p c j i", i=4),
            in_=q_raw[:, :, :CAST_SPLIT].rearrange("p j (c i) -> p c j i", i=4),
        )
        nc.scalar.activation(
            q_bf[:, CAST_SPLIT:, :].rearrange("p (c i) j -> p c j i", i=4),
            q_raw[:, :, CAST_SPLIT:].rearrange("p j (c i) -> p c j i", i=4),
            COPY,
        )
        q_codes = sb.tile([P, Q], U32, name="q_codes", align_bytes=64)
        q_scales = sb.tile([P, Q], U8, name="q_scales", align_bytes=64)
        nc.vector.quantize_mx(
            out=q_codes[:].bitcast(FP8X4),
            scales=q_scales[:],
            in_=q_bf[:].rearrange("p q j -> p (q j)"),
        )

        a = sb.tile([P, T], F32, name="a")
        first = 0
        for n, width in enumerate(MM_WIDTHS):
            cols = slice(first, first + width)
            first = first + width
            bank = ps.tile([P, width], F32, name="bank%d" % n)
            nc.tensor.matmul_mx(
                out=bank[:],
                lhsT=q_codes[:].bitcast(FP8X4),
                lhsT_scale=q_scales[:],
                rhs=k_words[:, 2 * cols.start : 2 * cols.stop].bitcast(FP4X4),
                rhs_scale=k_scales[:, cols],
                start=True,
                stop=True,
            )
            if n % 2 == 0:
                nc.scalar.activation(a[:, cols], bank[:], COPY)
            else:
                nc.vector.tensor_copy(out=a[:, cols], in_=bank[:])

        halves = [slice(h * HALF, (h + 1) * HALF) for h in range(2)]
        list_halves = [slice(h * HALF // PER_COLUMN, (h + 1) * HALF // PER_COLUMN) for h in range(2)]

        u = sb.tile([P, SLOTS], F32, name="u")
        v = sb.tile([P, SLOTS], F32, name="v")
        x = sb.tile([P, SLOTS], F32, name="x")
        x_lam = sb.tile([P, SLOTS], F32, name="x_lam")
        lean_col = sb.tile([P, 1], F32, name="lean_col")
        nc.gpsimd.tensor_scalar(lean_col[:], lam_col[:], -LEAN, 0.0, ALU.mult, ALU.add)
        for h in range(2):
            nc.vector.tensor_copy(u[:, halves[h]], a[:].indirect(list_u[:, list_halves[h]]))
            nc.scalar.activation(v[:, halves[h]], a[:].indirect(list_v[:, list_halves[h]]), COPY)
        for h in range(2):
            nc.scalar.activation(x[:, halves[h]], a[:].indirect(list_x[:, list_halves[h]]), COPY)
        for h in range(2):
            nc.scalar.activation(x_lam[:, halves[h]], x[:, halves[h]], COPY, scale=lam_col[:])

        larger = sb.tile([P, SLOTS], F32, name="larger")
        smaller = sb.tile([P, SLOTS], F32, name="smaller")
        capped = sb.tile([P, SLOTS], F32, name="capped")
        held = sb.tile([P, SLOTS], F32, name="held")
        lean = sb.tile([P, SLOTS], F32, name="lean")

        def pick(dst, s, op):
            nc.vector.tensor_tensor(dst[:, s], u[:, s], v[:, s], op)

        def cap(s):
            nc.vector.scalar_tensor_tensor(capped[:, s], larger[:, s], MARGIN, x[:, s], ALU.add, ALU.min)

        def hold(s):
            nc.vector.scalar_tensor_tensor(held[:, s], smaller[:, s], -MARGIN, capped[:, s], ALU.add, ALU.max)

        def put(h):
            s = halves[h]
            nc.vector.tensor_tensor(placed[:].indirect(list_put[:, list_halves[h]]), x_lam[:, s], lean[:, s], ALU.add)

        early, late = halves
        pick(larger, early, ALU.max)
        pick(smaller, early, ALU.min)
        pick(larger, late, ALU.max)
        cap(early)
        pick(smaller, late, ALU.min)
        hold(early)
        cap(late)
        nc.vector.tensor_scalar(lean[:, early], held[:, early], lam_col[:], -LEAN, ALU.mult, ALU.mult)
        hold(late)
        put(0)
        nc.scalar.activation(lean[:, late], held[:, late], COPY, scale=lean_col[:])
        put(1)

        total = sb.tile([P, T], F32, name="total")
        for n in range(T // N_OUT):
            cols = slice(n * N_OUT, (n + 1) * N_OUT)
            nc.vector.tensor_tensor(total[:, cols], placed[:, cols], old_sb[:, cols], ALU.add)
            nc.sync.dma_start(out=out[:, cols], in_=total[:, cols])
